import numpy as np
import ml_dtypes


def mxq(x, axis, fmt="e4m3"):
    dtype, down = {"e4m3": (ml_dtypes.float8_e4m3fn, 7), "e5m2": (ml_dtypes.float8_e5m2, 14)}[fmt]
    v = np.moveaxis(np.asarray(x, np.float32).astype(ml_dtypes.bfloat16).astype(np.float64), axis, -1)
    blocks = v.reshape(v.shape[:-1] + (-1, 32))
    amax = np.abs(blocks).max(-1, keepdims=True)
    byte = np.maximum(np.where(amax > 0, np.frexp(amax)[1] - 1 + 127, 0) - down, 1)
    scale = np.exp2(byte - 127.0)
    codes = (blocks / scale).astype(np.float32).astype(dtype).astype(np.float64)
    return np.moveaxis((codes * scale).reshape(v.shape), -1, axis)


WIDE = False


def mx_kscale(k):
    if not WIDE:
        return np.ones(k)
    levels = np.array([10, -10, 5, -5, 0])
    if k % 512:
        return np.exp2(np.random.permutation(np.resize(levels, k // 32))).repeat(32)
    a = np.empty((k // 512, 16))
    for p in range(k // 512):
        a[p, :8] = np.random.permutation(np.resize(levels, 8))
        for g in range(8):
            far = levels[np.abs(levels - a[p, g]) >= 10]
            a[p, g + 8] = far[np.random.randint(len(far))]
    return np.exp2(a.ravel()).repeat(32)


def f64(x):
    return np.asarray(x).astype(np.float64)


def striped(idx):
    return np.tile(idx.reshape(-1, 16).T, (8, 1)).astype(np.uint16)


def unstriped(offs):
    return offs[:16].T.reshape(-1).astype(np.int64)


E2M1 = np.array([0.0, 0.5, 1.0, 1.5, 2.0, 3.0, 4.0, 6.0, -0.0, -0.5, -1.0, -1.5, -2.0, -3.0, -4.0, -6.0])


def pack_weight(w, fmt):
    k, n = w.shape
    w = f64(np.asarray(w, np.float32).astype(ml_dtypes.bfloat16)).reshape(k // 32, 32, n)
    amax = np.abs(w).max(1)
    if fmt == "e4m3":
        byte = np.frexp(amax)[1] - 1 + 127 - 7
    else:
        mant, ex = np.frexp(amax / 6.0)
        byte = np.where(mant > 0.5, ex, ex - 1) + 127
    byte = np.clip(np.where(amax > 0, byte, 1), 1, 254)
    scaled = (w * np.exp2(127.0 - byte)[:, None, :]).reshape(k, n).astype(np.float32)
    by_word = np.ascontiguousarray(scaled.reshape(k // 512, 128, 4, n).transpose(0, 1, 3, 2))
    if fmt == "e4m3":
        words = by_word.astype(ml_dtypes.float8_e4m3fn).view(np.uint8)
    else:
        c = by_word.astype(ml_dtypes.float4_e2m1fn).view(np.uint8) & 0xF
        words = (c[..., 0::2] | (c[..., 1::2] << 4)).reshape(k // 512, 128, 2 * n)
    return np.ascontiguousarray(words), np.ascontiguousarray(byte.astype(np.uint8).reshape(k // 512, 16, n))


def unpack_weight(words, scales, fmt):
    g, _, n = scales.shape
    words = np.ascontiguousarray(words).reshape(g, 128, n, -1)
    if fmt == "e4m3":
        vals = words.view(ml_dtypes.float8_e4m3fn).astype(np.float64)
    else:
        nib = np.empty((g, 128, n, 4), np.uint8)
        nib[..., 0::2] = words & 0xF
        nib[..., 1::2] = words >> 4
        vals = E2M1[nib]
    vals = vals * np.repeat(np.exp2(scales.astype(np.float64) - 127.0), 8, axis=1)[..., None]
    return vals.transpose(0, 1, 3, 2).reshape(g * 512, n)


def gelu(v):
    return 0.5 * v * (1.0 + np.tanh(np.sqrt(2.0 / np.pi) * (v + 0.044715 * v**3)))


K, T, S, H, T3, S2, T2, P = 1024, 2048, 512, 512, 2048, 1024, 1024, 512


def setup_inputs():
    n = np.random.standard_normal
    s = mx_kscale(K)[:, None]
    u = mx_kscale(H)[:, None]
    tab_words, tab_scales = pack_weight(n((K, T)) * s, "e4m3")
    tab2_words, tab2_scales = pack_weight(n((H, T3)) / u / np.sqrt(H), "e4m3")
    w1 = (n((K, H)) / np.sqrt(K) / s * u.T).astype(np.float32)
    w3 = (0.8 * n((K, H)) / np.sqrt(K) / s * u.T).astype(np.float32)
    w4_words, w4_scales = pack_weight(n((K, H)) / np.sqrt(K) / s * u.T, "e2m1")
    return {
        "tab_words": tab_words, "tab_scales": tab_scales,
        "tab2_words": tab2_words, "tab2_scales": tab2_scales,
        "w1": w1, "w3": w3, "w4_words": w4_words, "w4_scales": w4_scales,
        "offs": striped(np.random.permutation(T)[:S]),
        "offs2": striped(np.random.permutation(T3)[:S2]),
        "offs3": striped(np.random.permutation(T2)[:S]),
        "pos1": striped(np.random.permutation(T2)[:P]),
        "pos2": striped(np.random.permutation(T2)[:P]),
        "wgs": np.exp(0.3 * n((128, S))).astype(np.float32),
        "page0": (n((H, T2)) * u).astype(np.float32),
        "conv": (0.8 * n((H, T2)) * u).astype(np.float32),
        "gm": n((S2, P)).astype(np.float32),
        "pv": (0.8 * n(S2)).astype(np.float32),
    }


def reference(tab_words, tab_scales, tab2_words, tab2_scales, w1, w3, w4_words, w4_scales,
              offs, offs2, offs3, pos1, pos2, wgs, page0, conv, gm, pv):
    v = unpack_weight(tab_words, tab_scales, "e4m3")[:, unstriped(offs)]
    v2 = unpack_weight(tab2_words, tab2_scales, "e4m3")[:, unstriped(offs2)]
    w4 = unpack_weight(w4_words, w4_scales, "e2m1")
    f1 = mxq(f64(w1), 0, "e4m3").T @ v
    f2 = w4.T @ v
    f3 = mxq(f64(w3), 0, "e4m3").T @ v
    h = np.minimum(f1, f2) + f3
    page = f64(page0).copy()
    page[:, unstriped(offs3)] = np.tile(f64(wgs), (H // 128, 1)) * h
    x = mxq(page + f64(conv), 0, "e4m3")
    e = v2.T @ x
    top = np.maximum(e[:, unstriped(pos1)], e[:, unstriped(pos2)])
    return top * f64(gm) + f64(pv)[:, None]

@@ -1,0 +1,297 @@
+from contextlib import ExitStack
+
+import concourse.mybir as mybir
+from concourse.masks import make_identity
+
+K, T, S, H, T3, S2, T2, PAIRS = 1024, 2048, 512, 512, 2048, 1024, 1024, 512
+FLOPS = 3 * 2 * K * H * S + 2 * H * S2 * T2
+
+F32 = mybir.dt.float32
+BF16 = mybir.dt.bfloat16
+I32 = mybir.dt.int32
+U32 = mybir.dt.uint32
+U16 = mybir.dt.uint16
+U8 = mybir.dt.uint8
+FP8X4 = mybir.dt.float8_e4m3fn_x4
+FP4X4 = mybir.dt.float4_e2m1fn_x4
+ALU = mybir.AluOpType
+IDENTITY = mybir.ActivationFunctionType.Identity
+
+P = 128
+PACK = 4
+K_PASS = P * PACK
+PASSES = K // K_PASS
+R_TILES = H // P
+M_TILES = S2 // P
+BANK = 512
+QUADRANTS = 4
+LIVE = 4
+
+
+def tile_list_roof_support_chooser_kernel(
+    tc, tab_words, tab_scales, tab2_words, tab2_scales, w1, w3, w4_words, w4_scales,
+    offs, offs2, offs3, pos1, pos2, wgs, page0, conv, gm, pv, out,
+):
+    nc = tc.nc
+    with ExitStack() as ctx:
+        keep = ctx.enter_context(tc.tile_pool(name="keep", bufs=1))
+        ring = ctx.enter_context(tc.tile_pool(name="ring", bufs=2))
+        psum = ctx.enter_context(tc.psum_pool(name="psum", bufs=1))
+
+        def bank(number, shape, name):
+            return psum.tile(shape, F32, name=name, tag="bank%d" % number)
+
+        def load_list(source, name):
+            tile = keep.tile(list(source.shape), U16, name=name)
+            nc.sync.dma_start(tile[:], source)
+            return tile
+
+        def load_scales(queue, tile, source):
+            for q in range(QUADRANTS):
+                queue.dma_start(
+                    tile[32 * q : 32 * q + LIVE].bitcast(I32),
+                    source[:, LIVE * q : LIVE * q + LIVE, :].rearrange("a r t -> r a t").bitcast(I32),
+                )
+
+        def load_words(source, name):
+            tile = keep.tile([P, source.shape[1]], U32, name=name, align_bytes=64)
+            nc.sync.dma_start(tile[:].bitcast(I32), source.rearrange("p t i -> p (t i)").bitcast(I32))
+            return tile
+
+        def load_rows(source, t, name):
+            tile = keep.tile([P, source.shape[1]], F32, name=name, align_bytes=64)
+            nc.sync.dma_start(tile[:], source[P * t : P * (t + 1), :])
+            return tile
+
+        raw_w = {}
+
+        def load_w(a, t0, tiles):
+            for i, w in enumerate((w1, w3)):
+                raw = keep.tile([P, PACK, P * tiles], F32, name="raw%d_%d_%d" % (t0, a, i), align_bytes=64)
+                nc.sync.dma_start(
+                    raw[:],
+                    w[K_PASS * a : K_PASS * (a + 1), P * t0 : P * (t0 + tiles)].rearrange("(p j) c -> p j c", j=PACK),
+                )
+                for t in range(tiles):
+                    raw_w[t0 + t, a, i] = raw[:, :, P * t : P * (t + 1)]
+
+        tab_sc = keep.tile([P, PASSES, T], U8, name="tab_sc", align_bytes=64)
+        w4_sc = keep.tile([P, PASSES, H], U8, name="w4_sc", align_bytes=64)
+        tab2_sc = keep.tile([P, 1, T3], U8, name="tab2_sc", align_bytes=64)
+        pv_rows = keep.tile([P, P], F32, name="pv_rows", align_bytes=64)
+        nc.gpsimd.memset(tab_sc[:, 0, :].bitcast(I32), 0)
+        nc.vector.memset(tab_sc[:, 1, :].bitcast(I32), 0)
+        nc.vector.memset(w4_sc[:].bitcast(I32), 0)
+        nc.vector.memset(tab2_sc[:].bitcast(I32), 0)
+        nc.vector.memset(pv_rows[:], 0.0)
+
+        offs_t = load_list(offs, "offs_t")
+        tab_w = [load_words(tab_words[0], "tab_w0")]
+        load_scales(nc.sync, tab_sc, tab_scales)
+        ident = keep.tile([P, P], F32, name="ident", align_bytes=64)
+        make_identity(nc, ident[:])
+        load_w(0, 0, 1)
+        tab_w.append(load_words(tab_words[1], "tab_w1"))
+        w4_w = keep.tile([P, PASSES, 2 * H], U8, name="w4_w", align_bytes=64)
+        nc.sync.dma_start(w4_w[:].bitcast(I32), w4_words.rearrange("a p c -> p a c").bitcast(I32))
+        load_scales(nc.sync, w4_sc, w4_scales)
+        load_w(1, 0, 1)
+        load_w(0, 1, 1)
+        load_w(1, 1, 1)
+        offs3_t = load_list(offs3, "offs3_t")
+        wgs_t = load_rows(wgs, 0, "wgs_t")
+        pages = [load_rows(page0, 0, "page_0")]
+        for t in range(2, R_TILES):
+            for a in range(PASSES):
+                load_w(a, t, 1)
+            pages.append(load_rows(page0, t - 1, "page_%d" % (t - 1)))
+        pages.append(load_rows(page0, 3, "page_3"))
+        convs = [load_rows(conv, t, "conv_%d" % t) for t in range(R_TILES - 1)]
+        nc.sync.dma_start(pv_rows[0:M_TILES, :], pv.rearrange("(i p) -> i p", p=P))
+        offs2_t = load_list(offs2, "offs2_t")
+        load_scales(nc.sync, tab2_sc, tab2_scales)
+        tab2_w = load_words(tab2_words[0], "tab2_w")
+        convs.append(load_rows(conv, R_TILES - 1, "conv_3"))
+        pos1_t = load_list(pos1, "pos1_t")
+        pos2_t = load_list(pos2, "pos2_t")
+        gms = [load_rows(gm, i, "gm_%d" % i) for i in range(M_TILES)]
+
+        v_sc = keep.tile([P, PASSES, S], U8, name="v_sc", align_bytes=64)
+        v_w = [keep.tile([P, S], U32, name="v_w%d" % a, align_bytes=64) for a in range(PASSES)]
+        for a in range(PASSES):
+            nc.vector.tensor_copy(v_sc[:, a, :], tab_sc[:, a, :].indirect(offs_t[:]))
+        nc.vector.tensor_copy(v_w[0][:], tab_w[0][:].indirect(offs_t[:]))
+
+        def round_w(t, a, tag, engine):
+            stage = keep.tile([P, 2, P, PACK], BF16, name="stage%d_%d" % (t, a), tag=tag, align_bytes=64)
+            for i in range(2):
+                dst = stage[:, i].rearrange("p (c i) j -> p c j i", i=4)
+                src = raw_w[t, a, i].rearrange("p j (c i) -> p c j i", i=4)
+                if engine == "v":
+                    nc.vector.tensor_copy(dst, src)
+                else:
+                    nc.scalar.copy(dst, src)
+            return stage
+
+        w_mx = {}
+
+        def quantise_w(t, a, stage):
+            codes = keep.tile([P, 2, P], U32, name="w_codes%d_%d" % (t, a), align_bytes=64)
+            scales = keep.tile([P, 2, P], U8, name="w_scales%d_%d" % (t, a), align_bytes=64)
+            nc.vector.quantize_mx(
+                out=codes[:].rearrange("p s c -> p (s c)").bitcast(FP8X4),
+                scales=scales[:].rearrange("p s c -> p (s c)"),
+                in_=stage[:].rearrange("p s c j -> p (s c j)"),
+            )
+            w_mx[t, a] = (codes, scales)
+
+        def first_products(t):
+            base = 3 * (t % 2)
+            f2 = bank(base, [P, S], "f2_%d" % t)
+            f1 = bank(base + 1, [P, S], "f1_%d" % t)
+            f3 = bank(base + 2, [P, S], "f3_%d" % t)
+            def passes(f, stationary):
+                for a in range(PASSES):
+                    words, scales = stationary(a)
+                    nc.tensor.matmul_mx(
+                        out=f[:], lhsT=words, lhsT_scale=scales,
+                        rhs=v_w[a][:].bitcast(FP8X4), rhs_scale=v_sc[:, a, :],
+                        start=(a == 0), stop=(a == PASSES - 1),
+                    )
+
+            passes(f2, lambda a: (
+                w4_w[:, a, 2 * P * t : 2 * P * (t + 1)].bitcast(FP4X4), w4_sc[:, a, P * t : P * (t + 1)]
+            ))
+            for i, f in enumerate((f1, f3)):
+                passes(f, lambda a: (w_mx[t, a][0][:, i, :].bitcast(FP8X4), w_mx[t, a][1][:, i, :]))
+            return f1, f2, f3
+
+        x_rows = [
+            keep.tile([P, 4, 2, P, 2], BF16, name="x_rows%d" % half, align_bytes=64) for half in range(2)
+        ]
+
+        def add_conv(t):
+            for half in range(2):
+                fx = bank(6 + half, [P, 4, P], "fx%d_%d" % (t, half))
+                for j, src in enumerate((convs[t], pages[t])):
+                    for b in range(4):
+                        n0 = BANK * half + P * b
+                        nc.tensor.matmul(
+                            fx[:, b, :], src[:, n0 : n0 + P], ident[:],
+                            start=(j == 0 and b == 0), stop=(j == 1 and b == 3), is_transpose=True,
+                        )
+                nc.scalar.copy(
+                    x_rows[half][:, :, :, 32 * t : 32 * (t + 1), :],
+                    fx[:].rearrange("n b (q u e) -> n b u q e", u=2, e=2),
+                )
+
+        quantise_w(0, 0, round_w(0, 0, "even1", "s"))
+        nc.vector.tensor_copy(v_w[1][:], tab_w[1][:].indirect(offs_t[:]))
+        quantise_w(0, 1, round_w(0, 1, "slot1", "v"))
+        quantise_w(1, 0, round_w(1, 0, "even0", "v"))
+
+        for t in range(R_TILES):
+            f1, f2, f3 = first_products(t)
+            f2_sb = ring.tile([P, S], F32, name="f2_sb", bufs=1)
+            nc.scalar.copy(f2_sb[:], f2[:])
+            stages = {}
+            if t + 1 < R_TILES:
+                for a in range(PASSES):
+                    if (t + 1, a) not in w_mx:
+                        tag = "slot%d" % (t % 2) if a == PASSES - 1 else "even%d" % (t % 2)
+                        stages[a] = round_w(t + 1, a, tag, "s")
+            least = ring.tile([P, S], F32, name="least")
+            nc.vector.tensor_tensor(least[:], f1[:], f2_sb[:], ALU.min)
+            for a, stage in stages.items():
+                quantise_w(t + 1, a, stage)
+            h = keep.tile([P, S], F32, name="h%d" % t, tag="slot%d" % (t % 2), align_bytes=64)
+            nc.vector.tensor_tensor(h[:], f3[:], least[:], ALU.add)
+            nc.vector.tensor_tensor(pages[t][:].indirect(offs3_t[:]), h[:], wgs_t[:], ALU.mult)
+            if t == 2:
+                pv_ps = bank(6, [P, P], "pv_ps")
+                nc.tensor.transpose(pv_ps[:], pv_rows[:], ident[:])
+                pv_col = keep.tile([P, M_TILES], F32, name="pv_col")
+                nc.scalar.activation(pv_col[:], pv_ps[:, 0:M_TILES], IDENTITY)
+            add_conv(t)
+
+        g_w = keep.tile([P, S2], U32, name="g_w", align_bytes=64)
+        nc.vector.tensor_copy(g_w[:], tab2_w[:].indirect(offs2_t[:]))
+        g_sc = []
+
+        def gather_scales(part, tag):
+            picked = keep.tile([P, S2 // 2], U8, name="g_sc%d" % part, tag=tag, align_bytes=64)
+            columns = S2 // 32
+            nc.vector.tensor_copy(
+                picked[:], tab2_sc[:, 0, :].indirect(offs2_t[:, columns * part : columns * (part + 1)])
+            )
+            g_sc.append(picked)
+
+        gather_scales(0, "g_sc0")
+
+        x_codes, x_scales = [], []
+        for half in range(2):
+            words = x_rows[half][:].rearrange("n b u p e -> n b u (p e)").bitcast(F32)
+            grouped = keep.tile([P, BANK, PACK], BF16, name="x_grouped%d" % half, tag="xg%d" % half, align_bytes=64)
+            for pair in range(2):
+                back = bank(2 * half + pair, [P, 2, 2, P], "back%d_%d" % (half, pair))
+                for u in range(2):
+                    for b in range(2):
+                        nc.tensor.transpose(back[:, u, b, :], words[:, 2 * pair + b, u, :], ident[:])
+                dst = grouped[:, 256 * pair : 256 * (pair + 1), :].bitcast(F32)
+                src = back[:].rearrange("p u b n -> p (b n) u")
+                nc.scalar.copy(dst, src)
+            codes = keep.tile([P, BANK], U32, name="x_codes%d" % half, align_bytes=64)
+            scales = keep.tile([P, BANK], U8, name="x_scales%d" % half, align_bytes=64)
+            nc.vector.quantize_mx(
+                out=codes[:].bitcast(FP8X4), scales=scales[:], in_=grouped[:].rearrange("p n j -> p (n j)")
+            )
+            x_codes.append(codes)
+            x_scales.append(scales)
+        gather_scales(1, "xg1")
+
+        def scores(i):
+            e = ring.tile([P, T2], F32, name="e", bufs=3)
+            for half in range(2):
+                ps = bank((4 + 2 * i + half) % 8, [P, BANK], "e_ps%d_%d" % (i, half))
+                nc.tensor.matmul_mx(
+                    out=ps[:],
+                    lhsT=g_w[:, P * i : P * (i + 1)].bitcast(FP8X4),
+                    lhsT_scale=g_sc[i // 4][:, P * (i % 4) : P * (i % 4 + 1)],
+                    rhs=x_codes[half][:].bitcast(FP8X4),
+                    rhs_scale=x_scales[half][:],
+                    start=True, stop=True,
+                )
+                nc.scalar.copy(e[:, BANK * half : BANK * (half + 1)], ps[:])
+            return e
+
+        def pick(e, positions, name):
+            picked = ring.tile([P, PAIRS], F32, name=name)
+            nc.vector.tensor_copy(picked[:], e[:].indirect(positions[:]))
+            return picked
+
+        def larger(first, second):
+            top = ring.tile([P, PAIRS], F32, name="top")
+            nc.vector.tensor_tensor(top[:], first[:], second[:], ALU.max)
+            return top
+
+        def finish(i, top):
+            weighted = ring.tile([P, PAIRS], F32, name="weighted")
+            nc.vector.tensor_tensor(weighted[:], top[:], gms[i][:], ALU.mult)
+            result = ring.tile([P, PAIRS], F32, name="result", bufs=3)
+            nc.scalar.activation(result[:], weighted[:], IDENTITY, bias=pv_col[:, i : i + 1])
+            nc.sync.dma_start(out[P * i : P * (i + 1), :], result[:])
+
+        e_next = scores(0)
+        held = None
+        for i in range(M_TILES):
+            e = e_next
+            if i + 1 < M_TILES:
+                e_next = scores(i + 1)
+            first = pick(e, pos1_t, "first")
+            if held is not None:
+                top = larger(*held)
+            second = pick(e, pos2_t, "second")
+            if held is not None:
+                finish(i - 1, top)
+            held = (first, second)
+        finish(M_TILES - 1, larger(*held))

@@ -38,8 +38,7 @@ def tile_list_roof_support_chooser_kernel(
         ring = ctx.enter_context(tc.tile_pool(name="ring", bufs=2))
         psum = ctx.enter_context(tc.psum_pool(name="psum", bufs=1))
 
-        def bank(number, shape, name):
-            return psum.tile(shape, F32, name=name, tag="bank%d" % number)
+        banks = [psum.tile([P, BANK], F32, name="bank%d" % number) for number in range(8)]
 
         def load_list(source, name):
             tile = keep.tile(list(source.shape), U16, name=name)
@@ -58,8 +57,8 @@ def tile_list_roof_support_chooser_kernel(
             nc.sync.dma_start(tile[:].bitcast(I32), source.rearrange("p t i -> p (t i)").bitcast(I32))
             return tile
 
-        def load_rows(source, t, name):
-            tile = keep.tile([P, source.shape[1]], F32, name=name, align_bytes=64)
+        def load_rows(source, t, name, tag=None):
+            tile = keep.tile([P, source.shape[1]], F32, name=name, tag=tag or name, align_bytes=64)
             nc.sync.dma_start(tile[:], source[P * t : P * (t + 1), :])
             return tile
 
@@ -82,16 +81,18 @@ def tile_list_roof_support_chooser_kernel(
         nc.gpsimd.memset(tab_sc[:, 0, :].bitcast(I32), 0)
         nc.vector.memset(tab_sc[:, 1, :].bitcast(I32), 0)
         nc.vector.memset(w4_sc[:].bitcast(I32), 0)
-        nc.vector.memset(tab2_sc[:].bitcast(I32), 0)
+        nc.gpsimd.memset(tab2_sc[:].bitcast(I32), 0)
         nc.vector.memset(pv_rows[:], 0.0)
 
         offs_t = load_list(offs, "offs_t")
         tab_w = [load_words(tab_words[0], "tab_w0")]
         load_scales(nc.sync, tab_sc, tab_scales)
+        load_scales(nc.gpsimd, tab2_sc, tab2_scales)
         ident = keep.tile([P, P], F32, name="ident", align_bytes=64)
         make_identity(nc, ident[:])
         load_w(0, 0, 1)
         tab_w.append(load_words(tab_words[1], "tab_w1"))
+        offs2_t = load_list(offs2, "offs2_t")
         w4_w = keep.tile([P, PASSES, 2 * H], U8, name="w4_w", align_bytes=64)
         nc.sync.dma_start(w4_w[:].bitcast(I32), w4_words.rearrange("a p c -> p a c").bitcast(I32))
         load_scales(nc.sync, w4_sc, w4_scales)
@@ -106,12 +107,9 @@ def tile_list_roof_support_chooser_kernel(
                 load_w(a, t, 1)
             pages.append(load_rows(page0, t - 1, "page_%d" % (t - 1)))
         pages.append(load_rows(page0, 3, "page_3"))
-        convs = [load_rows(conv, t, "conv_%d" % t) for t in range(R_TILES - 1)]
+        convs = [load_rows(conv, t, "conv_%d" % t) for t in range(R_TILES)]
         nc.sync.dma_start(pv_rows[0:M_TILES, :], pv.rearrange("(i p) -> i p", p=P))
-        offs2_t = load_list(offs2, "offs2_t")
-        load_scales(nc.sync, tab2_sc, tab2_scales)
         tab2_w = load_words(tab2_words[0], "tab2_w")
-        convs.append(load_rows(conv, R_TILES - 1, "conv_3"))
         pos1_t = load_list(pos1, "pos1_t")
         pos2_t = load_list(pos2, "pos2_t")
         gms = [load_rows(gm, i, "gm_%d" % i) for i in range(M_TILES)]
@@ -122,49 +120,63 @@ def tile_list_roof_support_chooser_kernel(
             nc.vector.tensor_copy(v_sc[:, a, :], tab_sc[:, a, :].indirect(offs_t[:]))
         nc.vector.tensor_copy(v_w[0][:], tab_w[0][:].indirect(offs_t[:]))
 
-        def round_w(t, a, tag, engine):
-            stage = keep.tile([P, 2, P, PACK], BF16, name="stage%d_%d" % (t, a), tag=tag, align_bytes=64)
-            for i in range(2):
-                dst = stage[:, i].rearrange("p (c i) j -> p c j i", i=4)
-                src = raw_w[t, a, i].rearrange("p j (c i) -> p c j i", i=4)
-                if engine == "v":
-                    nc.vector.tensor_copy(dst, src)
-                else:
-                    nc.scalar.copy(dst, src)
+        slots = [
+            keep.tile([P, PASSES * 2 * P * PACK], BF16, name="slot%d" % s, tag="slot%d" % s, align_bytes=64)
+            for s in range(2)
+        ]
+        early = [keep.tile([P, 2 * P * PACK], BF16, name="early%d" % s, align_bytes=64) for s in range(2)]
+
+        def round_w(t, passes, buffer, engine):
+            stage = buffer[:, 0 : len(passes) * 2 * P * PACK].rearrange("p (s i c j) -> p s i c j", i=2, c=P, j=PACK)
+            for s, a in enumerate(passes):
+                for i in range(2):
+                    dst = stage[:, s, i].rearrange("p (c i) j -> p c j i", i=4)
+                    src = raw_w[t, a, i].rearrange("p j (c i) -> p c j i", i=4)
+                    if engine == "v":
+                        nc.vector.tensor_copy(dst, src)
+                    else:
+                        nc.scalar.copy(dst, src)
             return stage
 
         w_mx = {}
 
-        def quantise_w(t, a, stage):
-            codes = keep.tile([P, 2, P], U32, name="w_codes%d_%d" % (t, a), align_bytes=64)
-            scales = keep.tile([P, 2, P], U8, name="w_scales%d_%d" % (t, a), align_bytes=64)
+        def quantise_w(t, passes, stage):
+            shape = [P, len(passes), 2, P]
+            codes = keep.tile(shape, U32, name="w_codes%d_%d" % (t, passes[0]), align_bytes=64)
+            scales = keep.tile(shape, U8, name="w_scales%d_%d" % (t, passes[0]), align_bytes=64)
             nc.vector.quantize_mx(
-                out=codes[:].rearrange("p s c -> p (s c)").bitcast(FP8X4),
-                scales=scales[:].rearrange("p s c -> p (s c)"),
-                in_=stage[:].rearrange("p s c j -> p (s c j)"),
+                out=codes[:].rearrange("p s i c -> p (s i c)").bitcast(FP8X4),
+                scales=scales[:].rearrange("p s i c -> p (s i c)"),
+                in_=stage.rearrange("p s i c j -> p (s i c j)"),
             )
-            w_mx[t, a] = (codes, scales)
+            for s, a in enumerate(passes):
+                w_mx[t, a] = (codes[:, s], scales[:, s])
 
-        def first_products(t):
-            base = 3 * (t % 2)
-            f2 = bank(base, [P, S], "f2_%d" % t)
-            f1 = bank(base + 1, [P, S], "f1_%d" % t)
-            f3 = bank(base + 2, [P, S], "f3_%d" % t)
-            def passes(f, stationary):
-                for a in range(PASSES):
-                    words, scales = stationary(a)
-                    nc.tensor.matmul_mx(
-                        out=f[:], lhsT=words, lhsT_scale=scales,
-                        rhs=v_w[a][:].bitcast(FP8X4), rhs_scale=v_sc[:, a, :],
-                        start=(a == 0), stop=(a == PASSES - 1),
-                    )
+        def first_product(f, stationary):
+            for a in range(PASSES):
+                words, scales = stationary(a)
+                nc.tensor.matmul_mx(
+                    out=f[:], lhsT=words, lhsT_scale=scales,
+                    rhs=v_w[a][:].bitcast(FP8X4), rhs_scale=v_sc[:, a, :],
+                    start=(a == 0), stop=(a == PASSES - 1),
+                )
 
-            passes(f2, lambda a: (
+        f2_sb = []
+
+        def w4_product(t):
+            f2 = banks[t]
+            first_product(f2, lambda a: (
                 w4_w[:, a, 2 * P * t : 2 * P * (t + 1)].bitcast(FP4X4), w4_sc[:, a, P * t : P * (t + 1)]
             ))
-            for i, f in enumerate((f1, f3)):
-                passes(f, lambda a: (w_mx[t, a][0][:, i, :].bitcast(FP8X4), w_mx[t, a][1][:, i, :]))
-            return f1, f2, f3
+            kept = keep.tile([P, S], F32, name="f2_sb%d" % t)
+            nc.scalar.copy(kept[:], f2[:])
+            f2_sb.append(kept)
+
+        def w1_w3_products(t):
+            pair = banks[4 + 2 * (t % 2) : 6 + 2 * (t % 2)]
+            for i, f in reversed(list(enumerate(pair))) if t else enumerate(pair):
+                first_product(f, lambda a: (w_mx[t, a][0][:, i, :].bitcast(FP8X4), w_mx[t, a][1][:, i, :]))
+            return pair
 
         x_rows = [
             keep.tile([P, 4, 2, P, 2], BF16, name="x_rows%d" % half, align_bytes=64) for half in range(2)
@@ -172,7 +184,7 @@ def tile_list_roof_support_chooser_kernel(
 
         def add_conv(t):
             for half in range(2):
-                fx = bank(6 + half, [P, 4, P], "fx%d_%d" % (t, half))
+                fx = banks[(0, 4, 0, 2)[t] + half][:].rearrange("n (b r) -> n b r", b=4)
                 for j, src in enumerate((convs[t], pages[t])):
                     for b in range(4):
                         n0 = BANK * half + P * b
@@ -182,116 +194,126 @@ def tile_list_roof_support_chooser_kernel(
                         )
                 nc.scalar.copy(
                     x_rows[half][:, :, :, 32 * t : 32 * (t + 1), :],
-                    fx[:].rearrange("n b (q u e) -> n b u q e", u=2, e=2),
+                    fx.rearrange("n b (q u e) -> n b u q e", u=2, e=2),
                 )
 
-        quantise_w(0, 0, round_w(0, 0, "even1", "s"))
+        quantise_w(0, [0], round_w(0, [0], early[0], "s"))
         nc.vector.tensor_copy(v_w[1][:], tab_w[1][:].indirect(offs_t[:]))
-        quantise_w(0, 1, round_w(0, 1, "slot1", "v"))
-        quantise_w(1, 0, round_w(1, 0, "even0", "v"))
+        g_sc = keep.tile([P, S2], U8, name="g_sc", align_bytes=64)
+        nc.vector.tensor_copy(g_sc[:], tab2_sc[:, 0, :].indirect(offs2_t[:]))
+        quantise_w(0, [1], round_w(0, [1], slots[1], "v"))
+        quantise_w(1, [0], round_w(1, [0], early[1], "v"))
 
         for t in range(R_TILES):
-            f1, f2, f3 = first_products(t)
-            f2_sb = ring.tile([P, S], F32, name="f2_sb", bufs=1)
-            nc.scalar.copy(f2_sb[:], f2[:])
-            stages = {}
-            if t + 1 < R_TILES:
-                for a in range(PASSES):
-                    if (t + 1, a) not in w_mx:
-                        tag = "slot%d" % (t % 2) if a == PASSES - 1 else "even%d" % (t % 2)
-                        stages[a] = round_w(t + 1, a, tag, "s")
-            least = ring.tile([P, S], F32, name="least")
-            nc.vector.tensor_tensor(least[:], f1[:], f2_sb[:], ALU.min)
-            for a, stage in stages.items():
-                quantise_w(t + 1, a, stage)
-            h = keep.tile([P, S], F32, name="h%d" % t, tag="slot%d" % (t % 2), align_bytes=64)
-            nc.vector.tensor_tensor(h[:], f3[:], least[:], ALU.add)
-            nc.vector.tensor_tensor(pages[t][:].indirect(offs3_t[:]), h[:], wgs_t[:], ALU.mult)
-            if t == 2:
-                pv_ps = bank(6, [P, P], "pv_ps")
-                nc.tensor.transpose(pv_ps[:], pv_rows[:], ident[:])
+            if t == 0:
+                w4_product(0)
+            f1, f3 = w1_w3_products(t)
+            todo = [a for a in range(PASSES) if t + 1 < R_TILES and (t + 1, a) not in w_mx]
+            if todo:
+                stage = round_w(t + 1, todo, slots[t % 2], "s")
+            if t == 0:
+                for later in range(1, R_TILES):
+                    w4_product(later)
+            if t == R_TILES - 1:
+                nc.tensor.transpose(banks[2][:, 0:P], pv_rows[:], ident[:])
                 pv_col = keep.tile([P, M_TILES], F32, name="pv_col")
-                nc.scalar.activation(pv_col[:], pv_ps[:, 0:M_TILES], IDENTITY)
-            add_conv(t)
+                nc.scalar.activation(pv_col[:], banks[2][:, 0:M_TILES], IDENTITY)
+                for done in range(t):
+                    add_conv(done)
+            least = ring.tile([P, S], F32, name="least")[:]
+            nc.vector.tensor_tensor(least, f1[:], f2_sb[t][:], ALU.min)
+            if todo:
+                quantise_w(t + 1, todo, stage)
+            h = slots[t % 2][:, 0 : 2 * S].bitcast(F32)
+            nc.vector.tensor_tensor(h, f3[:], least, ALU.add)
+            nc.vector.tensor_tensor(pages[t][:].indirect(offs3_t[:]), h, wgs_t[:], ALU.mult)
+        add_conv(R_TILES - 1)
 
-        g_w = keep.tile([P, S2], U32, name="g_w", align_bytes=64)
-        nc.vector.tensor_copy(g_w[:], tab2_w[:].indirect(offs2_t[:]))
-        g_sc = []
+        g_w = []
 
-        def gather_scales(part, tag):
-            picked = keep.tile([P, S2 // 2], U8, name="g_sc%d" % part, tag=tag, align_bytes=64)
+        def gather_candidates(part, tag):
+            picked = keep.tile([P, S2 // 2], U32, name="g_w%d" % part, tag=tag, align_bytes=64)
             columns = S2 // 32
-            nc.vector.tensor_copy(
-                picked[:], tab2_sc[:, 0, :].indirect(offs2_t[:, columns * part : columns * (part + 1)])
-            )
-            g_sc.append(picked)
+            nc.vector.tensor_copy(picked[:], tab2_w[:].indirect(offs2_t[:, columns * part : columns * (part + 1)]))
+            g_w.append(picked)
 
-        gather_scales(0, "g_sc0")
+        gather_candidates(0, "slot1")
 
-        x_codes, x_scales = [], []
-        for half in range(2):
+        QUARTER = T2 // 4
+        x_codes = [keep.tile([P, BANK], U32, name="x_codes%d" % half, align_bytes=64) for half in range(2)]
+        x_scales = [keep.tile([P, BANK], U8, name="x_scales%d" % half, align_bytes=64) for half in range(2)]
+        for quarter in range(4):
+            half, pair = divmod(quarter, 2)
             words = x_rows[half][:].rearrange("n b u p e -> n b u (p e)").bitcast(F32)
-            grouped = keep.tile([P, BANK, PACK], BF16, name="x_grouped%d" % half, tag="xg%d" % half, align_bytes=64)
-            for pair in range(2):
-                back = bank(2 * half + pair, [P, 2, 2, P], "back%d_%d" % (half, pair))
-                for u in range(2):
-                    for b in range(2):
-                        nc.tensor.transpose(back[:, u, b, :], words[:, 2 * pair + b, u, :], ident[:])
-                dst = grouped[:, 256 * pair : 256 * (pair + 1), :].bitcast(F32)
-                src = back[:].rearrange("p u b n -> p (b n) u")
-                nc.scalar.copy(dst, src)
-            codes = keep.tile([P, BANK], U32, name="x_codes%d" % half, align_bytes=64)
-            scales = keep.tile([P, BANK], U8, name="x_scales%d" % half, align_bytes=64)
-            nc.vector.quantize_mx(
-                out=codes[:].bitcast(FP8X4), scales=scales[:], in_=grouped[:].rearrange("p n j -> p (n j)")
+            grouped = keep.tile(
+                [P, QUARTER, PACK], BF16, name="x_grouped%d" % quarter, tag="xg%d" % quarter, align_bytes=64
             )
-            x_codes.append(codes)
-            x_scales.append(scales)
-        gather_scales(1, "xg1")
+            back = banks[4 + quarter][:].rearrange("p (u b n) -> p u b n", u=2, b=2)
+            for u in range(2):
+                for b in range(2):
+                    nc.tensor.transpose(back[:, u, b, :], words[:, 2 * pair + b, u, :], ident[:])
+            src = back.rearrange("p u b n -> p (b n) u")
+            if quarter == 1:
+                nc.vector.tensor_copy(grouped[:].bitcast(F32), src)
+            else:
+                nc.scalar.copy(grouped[:].bitcast(F32), src)
+            columns = slice(QUARTER * pair, QUARTER * (pair + 1))
+            nc.vector.quantize_mx(
+                out=x_codes[half][:, columns].bitcast(FP8X4),
+                scales=x_scales[half][:, columns],
+                in_=grouped[:].rearrange("p n j -> p (n j)"),
+            )
+        gather_candidates(1, "xg3")
 
-        def scores(i):
-            e = ring.tile([P, T2], F32, name="e", bufs=3)
-            for half in range(2):
-                ps = bank((4 + 2 * i + half) % 8, [P, BANK], "e_ps%d_%d" % (i, half))
+        turn = []
+
+        def scores(i, width):
+            e = ring.tile([P, T2], F32, name="e", bufs=4)
+            for n0 in range(0, T2, width):
+                ps = banks[len(turn) % 8][:, 0:width]
+                turn.append(n0)
+                half, c0 = divmod(n0, BANK)
                 nc.tensor.matmul_mx(
-                    out=ps[:],
-                    lhsT=g_w[:, P * i : P * (i + 1)].bitcast(FP8X4),
-                    lhsT_scale=g_sc[i // 4][:, P * (i % 4) : P * (i % 4 + 1)],
-                    rhs=x_codes[half][:].bitcast(FP8X4),
-                    rhs_scale=x_scales[half][:],
+                    out=ps,
+                    lhsT=g_w[i // 4][:, P * (i % 4) : P * (i % 4 + 1)].bitcast(FP8X4),
+                    lhsT_scale=g_sc[:, P * i : P * (i + 1)],
+                    rhs=x_codes[half][:, c0 : c0 + width].bitcast(FP8X4),
+                    rhs_scale=x_scales[half][:, c0 : c0 + width],
                     start=True, stop=True,
                 )
-                nc.scalar.copy(e[:, BANK * half : BANK * (half + 1)], ps[:])
+                nc.scalar.copy(e[:, n0 : n0 + width], ps)
             return e
 
-        def pick(e, positions, name):
-            picked = ring.tile([P, PAIRS], F32, name=name)
-            nc.vector.tensor_copy(picked[:], e[:].indirect(positions[:]))
+        def pick(e, positions, name, j0, width):
+            picked = ring.tile([P, width], F32, name=name)
+            nc.vector.tensor_copy(picked[:], e[:].indirect(positions[:, j0 // 16 : (j0 + width) // 16]))
             return picked
 
         def larger(first, second):
-            top = ring.tile([P, PAIRS], F32, name="top")
+            top = ring.tile(list(first.shape), F32, name="top")
             nc.vector.tensor_tensor(top[:], first[:], second[:], ALU.max)
             return top
 
-        def finish(i, top):
-            weighted = ring.tile([P, PAIRS], F32, name="weighted")
-            nc.vector.tensor_tensor(weighted[:], top[:], gms[i][:], ALU.mult)
-            result = ring.tile([P, PAIRS], F32, name="result", bufs=3)
+        def finish(i, j0, width, top):
+            weighted = ring.tile([P, width], F32, name="weighted", bufs=3)
+            engine = nc.vector if i == M_TILES - 1 and j0 + width == PAIRS else nc.gpsimd
+            engine.tensor_tensor(weighted[:], top[:], gms[i][:, j0 : j0 + width], ALU.mult)
+            result = ring.tile([P, width], F32, name="result", bufs=3)
             nc.scalar.activation(result[:], weighted[:], IDENTITY, bias=pv_col[:, i : i + 1])
-            nc.sync.dma_start(out[P * i : P * (i + 1), :], result[:])
+            nc.sync.dma_start(out[P * i : P * (i + 1), j0 : j0 + width], result[:])
 
-        e_next = scores(0)
+        steps = [(i, 0, PAIRS) for i in range(M_TILES - 1)]
+        steps.extend((M_TILES - 1, j0, PAIRS // 2) for j0 in (0, PAIRS // 2))
+        es = {0: scores(0, QUARTER), 1: scores(1, BANK)}
         held = None
-        for i in range(M_TILES):
-            e = e_next
-            if i + 1 < M_TILES:
-                e_next = scores(i + 1)
-            first = pick(e, pos1_t, "first")
+        for i, j0, width in steps:
+            if i + 2 < M_TILES:
+                es[i + 2] = scores(i + 2, BANK)
+            first = pick(es[i], pos1_t, "first", j0, width)
             if held is not None:
-                top = larger(*held)
-            second = pick(e, pos2_t, "second")
+                top = larger(*held[3:])
+            second = pick(es[i], pos2_t, "second", j0, width)
             if held is not None:
-                finish(i - 1, top)
-            held = (first, second)
-        finish(M_TILES - 1, larger(*held))
+                finish(*held[:3], top)
+            held = (i, j0, width, first, second)
+        finish(*held[:3], larger(*held[3:]))

from contextlib import ExitStack

import concourse.mybir as mybir
from concourse.masks import make_identity

K, T, S, H, T3, S2, T2, PAIRS = 1024, 2048, 512, 512, 2048, 1024, 1024, 512
FLOPS = 3 * 2 * K * H * S + 2 * H * S2 * T2

F32 = mybir.dt.float32
BF16 = mybir.dt.bfloat16
I32 = mybir.dt.int32
U32 = mybir.dt.uint32
U16 = mybir.dt.uint16
U8 = mybir.dt.uint8
FP8X4 = mybir.dt.float8_e4m3fn_x4
FP4X4 = mybir.dt.float4_e2m1fn_x4
ALU = mybir.AluOpType
IDENTITY = mybir.ActivationFunctionType.Identity

P = 128
PACK = 4
K_PASS = P * PACK
PASSES = K // K_PASS
R_TILES = H // P
M_TILES = S2 // P
BANK = 512
QUADRANTS = 4
LIVE = 4


def tile_list_roof_support_chooser_kernel(
    tc, tab_words, tab_scales, tab2_words, tab2_scales, w1, w3, w4_words, w4_scales,
    offs, offs2, offs3, pos1, pos2, wgs, page0, conv, gm, pv, out,
):
    nc = tc.nc
    with ExitStack() as ctx:
        keep = ctx.enter_context(tc.tile_pool(name="keep", bufs=1))
        ring = ctx.enter_context(tc.tile_pool(name="ring", bufs=2))
        psum = ctx.enter_context(tc.psum_pool(name="psum", bufs=1))

        banks = [psum.tile([P, BANK], F32, name="bank%d" % number) for number in range(8)]

        def load_list(source, name):
            tile = keep.tile(list(source.shape), U16, name=name)
            nc.sync.dma_start(tile[:], source)
            return tile

        def load_scales(queue, tile, source):
            for q in range(QUADRANTS):
                queue.dma_start(
                    tile[32 * q : 32 * q + LIVE].bitcast(I32),
                    source[:, LIVE * q : LIVE * q + LIVE, :].rearrange("a r t -> r a t").bitcast(I32),
                )

        def load_words(source, name):
            tile = keep.tile([P, source.shape[1]], U32, name=name, align_bytes=64)
            nc.sync.dma_start(tile[:].bitcast(I32), source.rearrange("p t i -> p (t i)").bitcast(I32))
            return tile

        def load_rows(source, t, name, tag=None):
            tile = keep.tile([P, source.shape[1]], F32, name=name, tag=tag or name, align_bytes=64)
            nc.sync.dma_start(tile[:], source[P * t : P * (t + 1), :])
            return tile

        raw_w = {}

        def load_w(a, t0, tiles):
            for i, w in enumerate((w1, w3)):
                raw = keep.tile([P, PACK, P * tiles], F32, name="raw%d_%d_%d" % (t0, a, i), align_bytes=64)
                nc.sync.dma_start(
                    raw[:],
                    w[K_PASS * a : K_PASS * (a + 1), P * t0 : P * (t0 + tiles)].rearrange("(p j) c -> p j c", j=PACK),
                )
                for t in range(tiles):
                    raw_w[t0 + t, a, i] = raw[:, :, P * t : P * (t + 1)]

        tab_sc = keep.tile([P, PASSES, T], U8, name="tab_sc", align_bytes=64)
        w4_sc = keep.tile([P, PASSES, H], U8, name="w4_sc", align_bytes=64)
        tab2_sc = keep.tile([P, 1, T3], U8, name="tab2_sc", align_bytes=64)
        pv_rows = keep.tile([P, P], F32, name="pv_rows", align_bytes=64)
        nc.gpsimd.memset(tab_sc[:, 0, :].bitcast(I32), 0)
        nc.vector.memset(tab_sc[:, 1, :].bitcast(I32), 0)
        nc.vector.memset(w4_sc[:].bitcast(I32), 0)
        nc.gpsimd.memset(tab2_sc[:].bitcast(I32), 0)
        nc.vector.memset(pv_rows[:], 0.0)

        offs_t = load_list(offs, "offs_t")
        tab_w = [load_words(tab_words[0], "tab_w0")]
        load_scales(nc.sync, tab_sc, tab_scales)
        load_scales(nc.gpsimd, tab2_sc, tab2_scales)
        ident = keep.tile([P, P], F32, name="ident", align_bytes=64)
        make_identity(nc, ident[:])
        load_w(0, 0, 1)
        tab_w.append(load_words(tab_words[1], "tab_w1"))
        offs2_t = load_list(offs2, "offs2_t")
        w4_w = keep.tile([P, PASSES, 2 * H], U8, name="w4_w", align_bytes=64)
        nc.sync.dma_start(w4_w[:].bitcast(I32), w4_words.rearrange("a p c -> p a c").bitcast(I32))
        load_scales(nc.sync, w4_sc, w4_scales)
        load_w(1, 0, 1)
        load_w(0, 1, 1)
        load_w(1, 1, 1)
        offs3_t = load_list(offs3, "offs3_t")
        wgs_t = load_rows(wgs, 0, "wgs_t")
        pages = [load_rows(page0, 0, "page_0")]
        for t in range(2, R_TILES):
            for a in range(PASSES):
                load_w(a, t, 1)
            pages.append(load_rows(page0, t - 1, "page_%d" % (t - 1)))
        pages.append(load_rows(page0, 3, "page_3"))
        convs = [load_rows(conv, t, "conv_%d" % t) for t in range(R_TILES)]
        nc.sync.dma_start(pv_rows[0:M_TILES, :], pv.rearrange("(i p) -> i p", p=P))
        tab2_w = load_words(tab2_words[0], "tab2_w")
        pos1_t = load_list(pos1, "pos1_t")
        pos2_t = load_list(pos2, "pos2_t")
        gms = [load_rows(gm, i, "gm_%d" % i) for i in range(M_TILES)]

        v_sc = keep.tile([P, PASSES, S], U8, name="v_sc", align_bytes=64)
        v_w = [keep.tile([P, S], U32, name="v_w%d" % a, align_bytes=64) for a in range(PASSES)]
        for a in range(PASSES):
            nc.vector.tensor_copy(v_sc[:, a, :], tab_sc[:, a, :].indirect(offs_t[:]))
        nc.vector.tensor_copy(v_w[0][:], tab_w[0][:].indirect(offs_t[:]))

        slots = [
            keep.tile([P, PASSES * 2 * P * PACK], BF16, name="slot%d" % s, tag="slot%d" % s, align_bytes=64)
            for s in range(2)
        ]
        early = [keep.tile([P, 2 * P * PACK], BF16, name="early%d" % s, align_bytes=64) for s in range(2)]

        def round_w(t, passes, buffer, engine):
            stage = buffer[:, 0 : len(passes) * 2 * P * PACK].rearrange("p (s i c j) -> p s i c j", i=2, c=P, j=PACK)
            for s, a in enumerate(passes):
                for i in range(2):
                    dst = stage[:, s, i].rearrange("p (c i) j -> p c j i", i=4)
                    src = raw_w[t, a, i].rearrange("p j (c i) -> p c j i", i=4)
                    if engine == "v":
                        nc.vector.tensor_copy(dst, src)
                    else:
                        nc.scalar.copy(dst, src)
            return stage

        w_mx = {}

        def quantise_w(t, passes, stage):
            shape = [P, len(passes), 2, P]
            codes = keep.tile(shape, U32, name="w_codes%d_%d" % (t, passes[0]), align_bytes=64)
            scales = keep.tile(shape, U8, name="w_scales%d_%d" % (t, passes[0]), align_bytes=64)
            nc.vector.quantize_mx(
                out=codes[:].rearrange("p s i c -> p (s i c)").bitcast(FP8X4),
                scales=scales[:].rearrange("p s i c -> p (s i c)"),
                in_=stage.rearrange("p s i c j -> p (s i c j)"),
            )
            for s, a in enumerate(passes):
                w_mx[t, a] = (codes[:, s], scales[:, s])

        def first_product(f, stationary):
            for a in range(PASSES):
                words, scales = stationary(a)
                nc.tensor.matmul_mx(
                    out=f[:], lhsT=words, lhsT_scale=scales,
                    rhs=v_w[a][:].bitcast(FP8X4), rhs_scale=v_sc[:, a, :],
                    start=(a == 0), stop=(a == PASSES - 1),
                )

        f2_sb = []

        def w4_product(t):
            f2 = banks[t]
            first_product(f2, lambda a: (
                w4_w[:, a, 2 * P * t : 2 * P * (t + 1)].bitcast(FP4X4), w4_sc[:, a, P * t : P * (t + 1)]
            ))
            kept = keep.tile([P, S], F32, name="f2_sb%d" % t)
            nc.scalar.copy(kept[:], f2[:])
            f2_sb.append(kept)

        def w1_w3_products(t):
            pair = banks[4 + 2 * (t % 2) : 6 + 2 * (t % 2)]
            for i, f in reversed(list(enumerate(pair))) if t else enumerate(pair):
                first_product(f, lambda a: (w_mx[t, a][0][:, i, :].bitcast(FP8X4), w_mx[t, a][1][:, i, :]))
            return pair

        x_rows = [
            keep.tile([P, 4, 2, P, 2], BF16, name="x_rows%d" % half, align_bytes=64) for half in range(2)
        ]

        def add_conv(t):
            for half in range(2):
                fx = banks[(0, 4, 0, 2)[t] + half][:].rearrange("n (b r) -> n b r", b=4)
                for j, src in enumerate((convs[t], pages[t])):
                    for b in range(4):
                        n0 = BANK * half + P * b
                        nc.tensor.matmul(
                            fx[:, b, :], src[:, n0 : n0 + P], ident[:],
                            start=(j == 0 and b == 0), stop=(j == 1 and b == 3), is_transpose=True,
                        )
                nc.scalar.copy(
                    x_rows[half][:, :, :, 32 * t : 32 * (t + 1), :],
                    fx.rearrange("n b (q u e) -> n b u q e", u=2, e=2),
                )

        quantise_w(0, [0], round_w(0, [0], early[0], "s"))
        nc.vector.tensor_copy(v_w[1][:], tab_w[1][:].indirect(offs_t[:]))
        g_sc = keep.tile([P, S2], U8, name="g_sc", align_bytes=64)
        nc.vector.tensor_copy(g_sc[:], tab2_sc[:, 0, :].indirect(offs2_t[:]))
        quantise_w(0, [1], round_w(0, [1], slots[1], "v"))
        quantise_w(1, [0], round_w(1, [0], early[1], "v"))

        for t in range(R_TILES):
            if t == 0:
                w4_product(0)
            f1, f3 = w1_w3_products(t)
            todo = [a for a in range(PASSES) if t + 1 < R_TILES and (t + 1, a) not in w_mx]
            if todo:
                stage = round_w(t + 1, todo, slots[t % 2], "s")
            if t == 0:
                for later in range(1, R_TILES):
                    w4_product(later)
            if t == R_TILES - 1:
                nc.tensor.transpose(banks[2][:, 0:P], pv_rows[:], ident[:])
                pv_col = keep.tile([P, M_TILES], F32, name="pv_col")
                nc.scalar.activation(pv_col[:], banks[2][:, 0:M_TILES], IDENTITY)
                for done in range(t):
                    add_conv(done)
            least = ring.tile([P, S], F32, name="least")[:]
            nc.vector.tensor_tensor(least, f1[:], f2_sb[t][:], ALU.min)
            if todo:
                quantise_w(t + 1, todo, stage)
            h = slots[t % 2][:, 0 : 2 * S].bitcast(F32)
            nc.vector.tensor_tensor(h, f3[:], least, ALU.add)
            nc.vector.tensor_tensor(pages[t][:].indirect(offs3_t[:]), h, wgs_t[:], ALU.mult)
        add_conv(R_TILES - 1)

        g_w = []

        def gather_candidates(part, tag):
            picked = keep.tile([P, S2 // 2], U32, name="g_w%d" % part, tag=tag, align_bytes=64)
            columns = S2 // 32
            nc.vector.tensor_copy(picked[:], tab2_w[:].indirect(offs2_t[:, columns * part : columns * (part + 1)]))
            g_w.append(picked)

        gather_candidates(0, "slot1")

        QUARTER = T2 // 4
        x_codes = [keep.tile([P, BANK], U32, name="x_codes%d" % half, align_bytes=64) for half in range(2)]
        x_scales = [keep.tile([P, BANK], U8, name="x_scales%d" % half, align_bytes=64) for half in range(2)]
        for quarter in range(4):
            half, pair = divmod(quarter, 2)
            words = x_rows[half][:].rearrange("n b u p e -> n b u (p e)").bitcast(F32)
            grouped = keep.tile(
                [P, QUARTER, PACK], BF16, name="x_grouped%d" % quarter, tag="xg%d" % quarter, align_bytes=64
            )
            back = banks[4 + quarter][:].rearrange("p (u b n) -> p u b n", u=2, b=2)
            for u in range(2):
                for b in range(2):
                    nc.tensor.transpose(back[:, u, b, :], words[:, 2 * pair + b, u, :], ident[:])
            src = back.rearrange("p u b n -> p (b n) u")
            if quarter == 1:
                nc.vector.tensor_copy(grouped[:].bitcast(F32), src)
            else:
                nc.scalar.copy(grouped[:].bitcast(F32), src)
            columns = slice(QUARTER * pair, QUARTER * (pair + 1))
            nc.vector.quantize_mx(
                out=x_codes[half][:, columns].bitcast(FP8X4),
                scales=x_scales[half][:, columns],
                in_=grouped[:].rearrange("p n j -> p (n j)"),
            )
        gather_candidates(1, "xg3")

        turn = []

        def scores(i, width):
            e = ring.tile([P, T2], F32, name="e", bufs=4)
            for n0 in range(0, T2, width):
                ps = banks[len(turn) % 8][:, 0:width]
                turn.append(n0)
                half, c0 = divmod(n0, BANK)
                nc.tensor.matmul_mx(
                    out=ps,
                    lhsT=g_w[i // 4][:, P * (i % 4) : P * (i % 4 + 1)].bitcast(FP8X4),
                    lhsT_scale=g_sc[:, P * i : P * (i + 1)],
                    rhs=x_codes[half][:, c0 : c0 + width].bitcast(FP8X4),
                    rhs_scale=x_scales[half][:, c0 : c0 + width],
                    start=True, stop=True,
                )
                nc.scalar.copy(e[:, n0 : n0 + width], ps)
            return e

        def pick(e, positions, name, j0, width):
            picked = ring.tile([P, width], F32, name=name)
            nc.vector.tensor_copy(picked[:], e[:].indirect(positions[:, j0 // 16 : (j0 + width) // 16]))
            return picked

        def larger(first, second):
            top = ring.tile(list(first.shape), F32, name="top")
            nc.vector.tensor_tensor(top[:], first[:], second[:], ALU.max)
            return top

        def finish(i, j0, width, top):
            weighted = ring.tile([P, width], F32, name="weighted", bufs=3)
            engine = nc.vector if i == M_TILES - 1 and j0 + width == PAIRS else nc.gpsimd
            engine.tensor_tensor(weighted[:], top[:], gms[i][:, j0 : j0 + width], ALU.mult)
            result = ring.tile([P, width], F32, name="result", bufs=3)
            nc.scalar.activation(result[:], weighted[:], IDENTITY, bias=pv_col[:, i : i + 1])
            nc.sync.dma_start(out[P * i : P * (i + 1), j0 : j0 + width], result[:])

        steps = [(i, 0, PAIRS) for i in range(M_TILES - 1)]
        steps.extend((M_TILES - 1, j0, PAIRS // 2) for j0 in (0, PAIRS // 2))
        es = {0: scores(0, QUARTER), 1: scores(1, BANK)}
        held = None
        for i, j0, width in steps:
            if i + 2 < M_TILES:
                es[i + 2] = scores(i + 2, BANK)
            first = pick(es[i], pos1_t, "first", j0, width)
            if held is not None:
                top = larger(*held[3:])
            second = pick(es[i], pos2_t, "second", j0, width)
            if held is not None:
                finish(*held[:3], top)
            held = (i, j0, width, first, second)
        finish(*held[:3], larger(*held[3:]))
